import numpy as np, ml_dtypes
CORES = [1,2,5,7,57,58,61,63,73,74,77,79]
N = 12
import mx_ref
NC = 256
BF = ml_dtypes.bfloat16
def setup_inputs(rng):
    def f(*shape):
        return mx_ref.flush((rng.standard_normal(shape, dtype=np.float32) * np.exp2(rng.integers(-2, 3, shape[:-1] + (1,)))).astype(BF))
    return {"c": f(N, 128, 512), "x": f(N, 128, 4 * NC)}
def setup_inputs_blocks(rng):
    d = setup_inputs(rng)
    for k in ("c", "x"): d[k] = mx_ref.spread(d[k], rng, 2)
    return d
def setup_inputs_wide(rng):
    d = setup_inputs(rng)
    for k in ("c", "x"): d[k] = mx_ref.flush((d[k].astype(np.float32) * np.exp2(rng.integers(-8, 9, (N, 1, 1))).astype(np.float32)).astype(BF))
    return d
def setup_inputs_zeros(rng):
    d = setup_inputs(rng); v = d["x"].reshape(N, 128, -1, 4).copy()
    v[np.broadcast_to((rng.random((N, 1, v.shape[2], 1)) < 0.33), v.shape)] = 0
    d["x"] = v.reshape(d["x"].shape)
    return d
def reference(c, x):
    QC = [mx_ref.quantize(c[k]) for k in range(N)]; QX = [mx_ref.quantize(x[j]) for j in range(N)]
    y = np.zeros((N, 128, NC), np.float32)
    for r in range(N):
        for j in range(N):
            p = mx_ref.matmul(QC[(r - j) % N], QX[j])
            y[r] = p if j == 0 else y[r] + p
    return {"y": y}

@@ -1,0 +1,214 @@
+from concourse.bass import DstId, RemoteDMATransfer
+from concourse.mybir import dt
+
+N = 12
+SIM = 80
+WC, WX = 128, 256
+W = WC + WX
+
+SCRATCH = {
+    "cin": ("sbuf", [128, 4 * WC], "bfloat16"),
+    "xin": ("sbuf", [128, 4 * WX], "bfloat16"),
+    "q": ("sbuf", [128, N * W], "float8_e4m3fn_x4"),
+    "s": ("sbuf", [128, N * W], "uint8"),
+    "acc": ("psum", [128, 512], "float32"),
+    "out": ("sbuf", [128, WX], "float32"),
+}
+SEMAPHORES = ["ldc", "ldx", "qd", "mm", "cp", "st", "sent"] + [k + str(t) for k in "cp" for t in range(N)]
+
+LAND = {
+    "c": {("paired", "S0"): "H0", ("paired", "S1"): "H1", ("paired", "X0"): "R0", ("paired", "X1"): "R1",
+          ("lone", "X0a"): "R0", ("lone", "X1a"): "H0", ("lone", "X0b"): "H0", ("lone", "X1b"): "H1"},
+    "p": {("paired", "S0"): "R1", ("paired", "S1"): "R0", ("paired", "X0"): "R1", ("paired", "X1"): "R1",
+          ("lone", "X0a"): "R1", ("lone", "X1a"): "R0", ("lone", "X0b"): "R0", ("lone", "X1b"): "R0"},
+}
+RELAY = {
+    "c": {("lone", 0): "R1", ("lone", 1): "H1", ("paired", 0): "H1"},
+    "p": {("lone", 0): "R1", ("lone", 1): "H1", ("paired", 0): "H1"},
+}
+
+
+def _bits(mask):
+    return [b for b in range(mask.bit_length()) if (mask >> b) & 1]
+
+
+def build_plan(cores, topo):
+    rank = {c: i for i, c in enumerate(cores)}
+    chips = []
+    for c in cores:
+        if topo.chip(c) not in chips:
+            chips.append(topo.chip(c))
+    cls = {A: ("paired" if any(topo.same_plane(A, x) for x in chips) else "lone") for A in chips}
+    far = {A: [c for c in range(SIM) if topo.chip(c) != A and not topo.same_plane(A, topo.chip(c))][0] for A in chips}
+
+    def role(ch, d):
+        out = {}
+        for c in range(SIM):
+            if topo.chip(c) == ch and topo.die(c) == d:
+                out[("R" if c in rank else "H") + ("1" if topo.may_write(c, far[ch]) else "0")] = c
+        return out
+
+    def on(ch):
+        return [c for c in cores if topo.chip(c) == ch]
+
+    flows = []
+    for kind in "cp":
+        for t, o in enumerate(cores):
+            A, d = topo.chip(o), topo.die(o)
+            ro = role(A, d)
+            kids = {o: [s for s in on(A) if s != o]}
+            for B in chips:
+                if B == A:
+                    continue
+                src = ("S" if topo.same_plane(A, B) else "X") + ("1" if ro["R1"] == o else "0")
+                if cls[B] == "lone":
+                    src += "ab"[[x for x in chips if x != B].index(A)]
+                l = role(B, d)[LAND[kind][(cls[B], src)]]
+                if topo.may_write(o, l):
+                    kids[o].append(l)
+                else:
+                    r = ro[RELAY[kind][(cls[A], [x for x in chips if x != A].index(B))]]
+                    if r not in kids[o]:
+                        kids[o].append(r)
+                    kids.setdefault(r, []).append(l)
+                kids[l] = [s for s in on(B) if s != l]
+            flows.append((kind, t, o, kids))
+
+    need, est, entries, ownstage = {}, {}, {}, {}
+
+    def height(kids, c):
+        return 0 if not kids.get(c) else 1 + max(height(kids, k) for k in kids[c])
+
+    def walk(kind, key, kids, c, e, root):
+        ch = kids.get(c, [])
+        if not ch:
+            return
+        sem = kind + str(key)
+        off = [k for k in ch if topo.chip(k) != topo.chip(c)]
+        onc = [k for k in ch if topo.chip(k) == topo.chip(c)]
+        deep = [k for k in onc if height(kids, k) > 0]
+        leaf = [k for k in onc if height(kids, k) == 0]
+        anyoff = [x for x in range(SIM) if topo.chip(x) != topo.chip(c) and topo.may_write(c, x)][0]
+        anyon = [x for x in range(SIM) if topo.chip(x) == topo.chip(c) and x != c][0]
+        offb = _bits(topo.mask(c, anyoff))
+        allb = _bits(topo.mask(c, anyon))
+        onlyb = [b for b in allb if b not in offb]
+        lp = 1 if kind == "p" else 2
+        calls = []
+        if off:
+            wave = [(off, offb)]
+            if deep:
+                wave.append((deep, onlyb))
+            calls.append((0, wave))
+            if leaf:
+                calls.append((lp, [(leaf, onlyb if not deep else allb)]))
+        else:
+            if deep:
+                calls.append((0, [(deep, allb)]))
+            if leaf:
+                calls.append((lp, [(leaf, allb)]))
+        for pr, wave in calls:
+            for dsts, bl in wave:
+                for k in dsts:
+                    need[(k, sem)] = len(bl)
+                    ek = e + (1.0 if topo.chip(k) == topo.chip(c) else 1.6) + 0.5 * pr + (0.0 if c in rank else 0.8) \
+                        + (0.3 if kind == "p" else 0.0)
+                    est[(k, sem)] = ek
+                    walk(kind, key, kids, k, ek, root)
+        if c == root:
+            for pr, wave in calls:
+                ownstage.setdefault(c, []).append((pr, kind, key, wave))
+        else:
+            entries.setdefault(c, []).append((e, kind, key, [sem], [w for _, w in calls]))
+
+    for kind, key, root, kids in flows:
+        walk(kind, key, kids, root, 0.0, root)
+
+    prog = {}
+    for c in sorted(set(entries) | set(ownstage)):
+        seq = []
+        if c in ownstage:
+            seq.append(("wait", ["own"]))
+            for pr, kind, key, wave in sorted(ownstage[c], key=lambda x: x[0]):
+                seq.append(("call", kind, key, wave))
+        for e, kind, key, waits, waves in sorted(entries.get(c, []), key=lambda x: (x[0], x[1], x[2])):
+            seq.append(("wait", waits))
+            for wave in waves:
+                seq.append(("call", kind, key, wave))
+        prog[c] = seq
+    return prog, need, est
+
+
+def rank_program(g, core, T, topo):
+    cores = list(T.cores)
+    prog, need, est = build_plan(cores, topo)
+    r = T.rank_of(core)
+    if r is None and core not in prog:
+        return
+
+    def view(kind, t):
+        if kind == "c":
+            return T.q[:, t * W:(t + 1) * W].bitcast(dt.uint8)
+        return T.s[:, t * W:(t + 1) * W]
+
+    if r is not None:
+        a = r * W
+        g.sync.dma_start(T.cin[:], T.c[:]).then_inc(T.sem.ldc, 16)
+        g.scalar.dma_start(T.xin[:], T.x[:]).then_inc(T.sem.ldx, 16)
+        g.vector.wait_ge(T.sem.ldc, 16)
+        g.vector.quantize_mx(T.q[:, a:a + WC], T.s[:, a:a + WC], T.cin[:]).then_inc(T.sem.qd, 1)
+        g.vector.wait_ge(T.sem.ldx, 16)
+        g.vector.quantize_mx(T.q[:, a + WC:a + W], T.s[:, a + WC:a + W], T.xin[:]).then_inc(T.sem.qd, 1)
+
+    sent = 0
+    for op in prog.get(core, []):
+        if op[0] == "wait":
+            for name in op[1]:
+                if name == "own":
+                    g.wait_ge(T.sem.qd, 2)
+                else:
+                    g.wait_ge(T.sem[name], need[(core, name)])
+            continue
+        _, kind, t, wave = op
+        transfers = []
+        for dsts, bl in wave:
+            ids = []
+            for k in dsts:
+                rid, pid, _ = topo.addr(k)
+                ids.append(DstId(rid=rid, pnc=pid))
+            transfers.append(RemoteDMATransfer(dst_ids=ids, dma_engine_mask=sum(1 << b for b in bl),
+                                               remote_sem=T.sem[kind + str(t)], srcs=[view(kind, t)],
+                                               dsts=[view(kind, t) for _ in dsts]))
+            sent += len(bl)
+        g.remote_dma_fused(transfers, local_sem=T.sem.sent)
+    if sent:
+        g.wait_ge(T.sem.sent, sent)
+
+    if r is None:
+        return
+
+    def when(t):
+        return 0.0 if t == r else max(est[(core, "c" + str(t))], est[(core, "p" + str(t))])
+
+    order = sorted(range(N), key=lambda j: (max(when(j), when((r - j) % N)), j))
+    seen = set()
+    mm = None
+    for n, j in enumerate(order):
+        k = (r - j) % N
+        for t in (j, k):
+            if t in seen:
+                continue
+            seen.add(t)
+            if t == r:
+                g.tensor.wait_ge(T.sem.qd, 2)
+            else:
+                for kind in "cp":
+                    g.tensor.wait_ge(T.sem[kind + str(t)], need[(core, kind + str(t))])
+        mm = g.tensor.matmul_mx(T.acc[:, 0:WX], T.q[:, k * W:k * W + WC], T.s[:, k * W:k * W + WC],
+                                T.q[:, j * W + WC:(j + 1) * W], T.s[:, j * W + WC:(j + 1) * W], n == 0, n == N - 1)
+    mm.then_inc(T.sem.mm, 1)
+    g.vector.wait_ge(T.sem.mm, 1)
+    g.vector.tensor_copy(T.out[:], T.acc[:, 0:WX]).then_inc(T.sem.cp, 1)
+    g.sync.wait_ge(T.sem.cp, 1)
+    g.sync.dma_start(T.y[:], T.out[:]).then_inc(T.sem.st, 16)
+    g.sync.wait_ge(T.sem.st, 16)

@@ -5,6 +5,7 @@ N = 12
 SIM = 80
 WC, WX = 128, 256
 W = WC + WX
+KINDS = "apx"
 
 SCRATCH = {
     "cin": ("sbuf", [128, 4 * WC], "bfloat16"),
@@ -14,18 +15,12 @@ SCRATCH = {
     "acc": ("psum", [128, 512], "float32"),
     "out": ("sbuf", [128, WX], "float32"),
 }
-SEMAPHORES = ["ldc", "ldx", "qd", "mm", "cp", "st", "sent"] + [k + str(t) for k in "cp" for t in range(N)]
+SEMAPHORES = ["ldc", "ldx", "qc", "qx", "mm", "cp", "st", "sent"] + [k + str(t) for k in KINDS for t in range(N)]
 
-LAND = {
-    "c": {("paired", "S0"): "H0", ("paired", "S1"): "H1", ("paired", "X0"): "R0", ("paired", "X1"): "R1",
-          ("lone", "X0a"): "R0", ("lone", "X1a"): "H0", ("lone", "X0b"): "H0", ("lone", "X1b"): "H1"},
-    "p": {("paired", "S0"): "R1", ("paired", "S1"): "R0", ("paired", "X0"): "R1", ("paired", "X1"): "R1",
-          ("lone", "X0a"): "R1", ("lone", "X1a"): "R0", ("lone", "X0b"): "R0", ("lone", "X1b"): "R0"},
-}
-RELAY = {
-    "c": {("lone", 0): "R1", ("lone", 1): "H1", ("paired", 0): "H1"},
-    "p": {("lone", 0): "R1", ("lone", 1): "H1", ("paired", 0): "H1"},
-}
+LAND = {("paired", "S0"): "H0", ("paired", "S1"): "H1", ("paired", "X0"): "R0", ("paired", "X1"): "R1",
+        ("lone", "X0a"): "R0", ("lone", "X1a"): "H0", ("lone", "X0b"): "R1", ("lone", "X1b"): "H1"}
+RELAY = {("paired", "X0"): "M", ("lone", "X0a"): "H1", ("lone", "X0b"): "M"}
+LATER = {"a": 0.0, "p": 0.1, "x": 1.5}
 
 
 def _bits(mask):
@@ -39,6 +34,7 @@ def build_plan(cores, topo):
         if topo.chip(c) not in chips:
             chips.append(topo.chip(c))
     cls = {A: ("paired" if any(topo.same_plane(A, x) for x in chips) else "lone") for A in chips}
+    paired = [A for A in chips if cls[A] == "paired"]
     far = {A: [c for c in range(SIM) if topo.chip(c) != A and not topo.same_plane(A, topo.chip(c))][0] for A in chips}
 
     def role(ch, d):
@@ -52,22 +48,29 @@ def build_plan(cores, topo):
         return [c for c in cores if topo.chip(c) == ch]
 
     flows = []
-    for kind in "cp":
+    for kind in KINDS:
         for t, o in enumerate(cores):
             A, d = topo.chip(o), topo.die(o)
             ro = role(A, d)
             kids = {o: [s for s in on(A) if s != o]}
-            for B in chips:
-                if B == A:
-                    continue
-                src = ("S" if topo.same_plane(A, B) else "X") + ("1" if ro["R1"] == o else "0")
+            others = [x for x in chips if x != A]
+            mine = ro["R1"] == o
+            if (cls[A] == "lone" and not mine) or (cls[A] == "paired" and mine and paired.index(A) == 1):
+                others.reverse()
+            for B in others:
+                src = ("S" if topo.same_plane(A, B) else "X") + ("1" if mine else "0")
                 if cls[B] == "lone":
                     src += "ab"[[x for x in chips if x != B].index(A)]
-                l = role(B, d)[LAND[kind][(cls[B], src)]]
+                l = role(B, d)[LAND[(cls[B], src)]]
                 if topo.may_write(o, l):
                     kids[o].append(l)
                 else:
-                    r = ro[RELAY[kind][(cls[A], [x for x in chips if x != A].index(B))]]
+                    via = RELAY[(cls[B], src)]
+                    if via == "M":
+                        r = [c for c in range(SIM) if topo.mates(topo.chip(c), B) and topo.die(c) == d
+                             and topo.may_write(c, l)][0]
+                    else:
+                        r = ro[via]
                     if r not in kids[o]:
                         kids[o].append(r)
                     kids.setdefault(r, []).append(l)
@@ -93,33 +96,22 @@ def build_plan(cores, topo):
         offb = _bits(topo.mask(c, anyoff))
         allb = _bits(topo.mask(c, anyon))
         onlyb = [b for b in allb if b not in offb]
-        lp = 1 if kind == "p" else 2
-        calls = []
+        wave = []
         if off:
-            wave = [(off, offb)]
-            if deep:
-                wave.append((deep, onlyb))
-            calls.append((0, wave))
-            if leaf:
-                calls.append((lp, [(leaf, onlyb if not deep else allb)]))
-        else:
-            if deep:
-                calls.append((0, [(deep, allb)]))
-            if leaf:
-                calls.append((lp, [(leaf, allb)]))
-        for pr, wave in calls:
-            for dsts, bl in wave:
-                for k in dsts:
-                    need[(k, sem)] = len(bl)
-                    ek = e + (1.0 if topo.chip(k) == topo.chip(c) else 1.6) + 0.5 * pr + (0.0 if c in rank else 0.8) \
-                        + (0.3 if kind == "p" else 0.0)
-                    est[(k, sem)] = ek
-                    walk(kind, key, kids, k, ek, root)
+            wave.append((off, offb))
+        if deep + leaf:
+            wave.append((deep + leaf, onlyb if off else allb))
+        for dsts, bl in wave:
+            for n, k in enumerate(dsts):
+                need[(k, sem)] = len(bl)
+                ek = e + (1.0 if topo.chip(k) == topo.chip(c) else 1.6) + 0.2 * n + (0.0 if c in rank else 0.8) \
+                    + LATER[kind]
+                est[(k, sem)] = ek
+                walk(kind, key, kids, k, ek, root)
         if c == root:
-            for pr, wave in calls:
-                ownstage.setdefault(c, []).append((pr, kind, key, wave))
+            ownstage.setdefault(c, []).append((kind, key, wave))
         else:
-            entries.setdefault(c, []).append((e, kind, key, [sem], [w for _, w in calls]))
+            entries.setdefault(c, []).append((e, kind, key, [sem], wave))
 
     for kind, key, root, kids in flows:
         walk(kind, key, kids, root, 0.0, root)
@@ -127,14 +119,15 @@ def build_plan(cores, topo):
     prog = {}
     for c in sorted(set(entries) | set(ownstage)):
         seq = []
-        if c in ownstage:
-            seq.append(("wait", ["own"]))
-            for pr, kind, key, wave in sorted(ownstage[c], key=lambda x: x[0]):
-                seq.append(("call", kind, key, wave))
-        for e, kind, key, waits, waves in sorted(entries.get(c, []), key=lambda x: (x[0], x[1], x[2])):
+        for kind, key, wave in ownstage.get(c, []):
+            if kind == "a":
+                seq.append(("wait", ["ownc"]))
+            elif kind == "p":
+                seq.append(("wait", ["ownx"]))
+            seq.append(("call", kind, key, wave))
+        for e, kind, key, waits, wave in sorted(entries.get(c, []), key=lambda x: (x[0], x[1], x[2])):
             seq.append(("wait", waits))
-            for wave in waves:
-                seq.append(("call", kind, key, wave))
+            seq.append(("call", kind, key, wave))
         prog[c] = seq
     return prog, need, est
 
@@ -147,8 +140,10 @@ def rank_program(g, core, T, topo):
         return
 
     def view(kind, t):
-        if kind == "c":
-            return T.q[:, t * W:(t + 1) * W].bitcast(dt.uint8)
+        if kind == "a":
+            return T.q[:, t * W:t * W + WC].bitcast(dt.uint8)
+        if kind == "x":
+            return T.q[:, t * W + WC:(t + 1) * W].bitcast(dt.uint8)
         return T.s[:, t * W:(t + 1) * W]
 
     if r is not None:
@@ -156,16 +151,18 @@ def rank_program(g, core, T, topo):
         g.sync.dma_start(T.cin[:], T.c[:]).then_inc(T.sem.ldc, 16)
         g.scalar.dma_start(T.xin[:], T.x[:]).then_inc(T.sem.ldx, 16)
         g.vector.wait_ge(T.sem.ldc, 16)
-        g.vector.quantize_mx(T.q[:, a:a + WC], T.s[:, a:a + WC], T.cin[:]).then_inc(T.sem.qd, 1)
+        g.vector.quantize_mx(T.q[:, a:a + WC], T.s[:, a:a + WC], T.cin[:]).then_inc(T.sem.qc, 1)
         g.vector.wait_ge(T.sem.ldx, 16)
-        g.vector.quantize_mx(T.q[:, a + WC:a + W], T.s[:, a + WC:a + W], T.xin[:]).then_inc(T.sem.qd, 1)
+        g.vector.quantize_mx(T.q[:, a + WC:a + W], T.s[:, a + WC:a + W], T.xin[:]).then_inc(T.sem.qx, 1)
 
     sent = 0
     for op in prog.get(core, []):
         if op[0] == "wait":
             for name in op[1]:
-                if name == "own":
-                    g.wait_ge(T.sem.qd, 2)
+                if name == "ownc":
+                    g.wait_ge(T.sem.qc, 1)
+                elif name == "ownx":
+                    g.wait_ge(T.sem.qx, 1)
                 else:
                     g.wait_ge(T.sem[name], need[(core, name)])
             continue
@@ -187,23 +184,23 @@ def rank_program(g, core, T, topo):
     if r is None:
         return
 
-    def when(t):
-        return 0.0 if t == r else max(est[(core, "c" + str(t))], est[(core, "p" + str(t))])
+    def when(kind, t):
+        return 0.0 if t == r else max(est[(core, kind + str(t))], est[(core, "p" + str(t))])
 
-    order = sorted(range(N), key=lambda j: (max(when(j), when((r - j) % N)), j))
+    order = sorted(range(N), key=lambda j: (max(when("x", j), when("a", (r - j) % N)), j))
     seen = set()
     mm = None
     for n, j in enumerate(order):
         k = (r - j) % N
-        for t in (j, k):
-            if t in seen:
+        for name in ("a" + str(k), "p" + str(k), "x" + str(j), "p" + str(j)):
+            if name in seen:
                 continue
-            seen.add(t)
-            if t == r:
-                g.tensor.wait_ge(T.sem.qd, 2)
+            seen.add(name)
+            if name[1:] == str(r):
+                g.tensor.wait_ge(T.sem.qc, 1)
+                g.tensor.wait_ge(T.sem.qx, 1)
             else:
-                for kind in "cp":
-                    g.tensor.wait_ge(T.sem[kind + str(t)], need[(core, kind + str(t))])
+                g.tensor.wait_ge(T.sem[name], need[(core, name)])
         mm = g.tensor.matmul_mx(T.acc[:, 0:WX], T.q[:, k * W:k * W + WC], T.s[:, k * W:k * W + WC],
                                 T.q[:, j * W + WC:(j + 1) * W], T.s[:, j * W + WC:(j + 1) * W], n == 0, n == N - 1)
     mm.then_inc(T.sem.mm, 1)

from concourse.bass import DstId, RemoteDMATransfer
from concourse.mybir import dt

N = 12
SIM = 80
WC, WX = 128, 256
W = WC + WX
KINDS = "apx"

SCRATCH = {
    "cin": ("sbuf", [128, 4 * WC], "bfloat16"),
    "xin": ("sbuf", [128, 4 * WX], "bfloat16"),
    "q": ("sbuf", [128, N * W], "float8_e4m3fn_x4"),
    "s": ("sbuf", [128, N * W], "uint8"),
    "acc": ("psum", [128, 512], "float32"),
    "out": ("sbuf", [128, WX], "float32"),
}
SEMAPHORES = ["ldc", "ldx", "qc", "qx", "mm", "cp", "st", "sent"] + [k + str(t) for k in KINDS for t in range(N)]

LAND = {("paired", "S0"): "H0", ("paired", "S1"): "H1", ("paired", "X0"): "R0", ("paired", "X1"): "R1",
        ("lone", "X0a"): "R0", ("lone", "X1a"): "H0", ("lone", "X0b"): "R1", ("lone", "X1b"): "H1"}
RELAY = {("paired", "X0"): "M", ("lone", "X0a"): "H1", ("lone", "X0b"): "M"}
LATER = {"a": 0.0, "p": 0.1, "x": 1.5}


def _bits(mask):
    return [b for b in range(mask.bit_length()) if (mask >> b) & 1]


def build_plan(cores, topo):
    rank = {c: i for i, c in enumerate(cores)}
    chips = []
    for c in cores:
        if topo.chip(c) not in chips:
            chips.append(topo.chip(c))
    cls = {A: ("paired" if any(topo.same_plane(A, x) for x in chips) else "lone") for A in chips}
    paired = [A for A in chips if cls[A] == "paired"]
    far = {A: [c for c in range(SIM) if topo.chip(c) != A and not topo.same_plane(A, topo.chip(c))][0] for A in chips}

    def role(ch, d):
        out = {}
        for c in range(SIM):
            if topo.chip(c) == ch and topo.die(c) == d:
                out[("R" if c in rank else "H") + ("1" if topo.may_write(c, far[ch]) else "0")] = c
        return out

    def on(ch):
        return [c for c in cores if topo.chip(c) == ch]

    flows = []
    for kind in KINDS:
        for t, o in enumerate(cores):
            A, d = topo.chip(o), topo.die(o)
            ro = role(A, d)
            kids = {o: [s for s in on(A) if s != o]}
            others = [x for x in chips if x != A]
            mine = ro["R1"] == o
            if (cls[A] == "lone" and not mine) or (cls[A] == "paired" and mine and paired.index(A) == 1):
                others.reverse()
            for B in others:
                src = ("S" if topo.same_plane(A, B) else "X") + ("1" if mine else "0")
                if cls[B] == "lone":
                    src += "ab"[[x for x in chips if x != B].index(A)]
                l = role(B, d)[LAND[(cls[B], src)]]
                if topo.may_write(o, l):
                    kids[o].append(l)
                else:
                    via = RELAY[(cls[B], src)]
                    if via == "M":
                        r = [c for c in range(SIM) if topo.mates(topo.chip(c), B) and topo.die(c) == d
                             and topo.may_write(c, l)][0]
                    else:
                        r = ro[via]
                    if r not in kids[o]:
                        kids[o].append(r)
                    kids.setdefault(r, []).append(l)
                kids[l] = [s for s in on(B) if s != l]
            flows.append((kind, t, o, kids))

    need, est, entries, ownstage = {}, {}, {}, {}

    def height(kids, c):
        return 0 if not kids.get(c) else 1 + max(height(kids, k) for k in kids[c])

    def walk(kind, key, kids, c, e, root):
        ch = kids.get(c, [])
        if not ch:
            return
        sem = kind + str(key)
        off = [k for k in ch if topo.chip(k) != topo.chip(c)]
        onc = [k for k in ch if topo.chip(k) == topo.chip(c)]
        deep = [k for k in onc if height(kids, k) > 0]
        leaf = [k for k in onc if height(kids, k) == 0]
        anyoff = [x for x in range(SIM) if topo.chip(x) != topo.chip(c) and topo.may_write(c, x)][0]
        anyon = [x for x in range(SIM) if topo.chip(x) == topo.chip(c) and x != c][0]
        offb = _bits(topo.mask(c, anyoff))
        allb = _bits(topo.mask(c, anyon))
        onlyb = [b for b in allb if b not in offb]
        wave = []
        if off:
            wave.append((off, offb))
        if deep + leaf:
            wave.append((deep + leaf, onlyb if off else allb))
        for dsts, bl in wave:
            for n, k in enumerate(dsts):
                need[(k, sem)] = len(bl)
                ek = e + (1.0 if topo.chip(k) == topo.chip(c) else 1.6) + 0.2 * n + (0.0 if c in rank else 0.8) \
                    + LATER[kind]
                est[(k, sem)] = ek
                walk(kind, key, kids, k, ek, root)
        if c == root:
            ownstage.setdefault(c, []).append((kind, key, wave))
        else:
            entries.setdefault(c, []).append((e, kind, key, [sem], wave))

    for kind, key, root, kids in flows:
        walk(kind, key, kids, root, 0.0, root)

    prog = {}
    for c in sorted(set(entries) | set(ownstage)):
        seq = []
        for kind, key, wave in ownstage.get(c, []):
            if kind == "a":
                seq.append(("wait", ["ownc"]))
            elif kind == "p":
                seq.append(("wait", ["ownx"]))
            seq.append(("call", kind, key, wave))
        for e, kind, key, waits, wave in sorted(entries.get(c, []), key=lambda x: (x[0], x[1], x[2])):
            seq.append(("wait", waits))
            seq.append(("call", kind, key, wave))
        prog[c] = seq
    return prog, need, est


def rank_program(g, core, T, topo):
    cores = list(T.cores)
    prog, need, est = build_plan(cores, topo)
    r = T.rank_of(core)
    if r is None and core not in prog:
        return

    def view(kind, t):
        if kind == "a":
            return T.q[:, t * W:t * W + WC].bitcast(dt.uint8)
        if kind == "x":
            return T.q[:, t * W + WC:(t + 1) * W].bitcast(dt.uint8)
        return T.s[:, t * W:(t + 1) * W]

    if r is not None:
        a = r * W
        g.sync.dma_start(T.cin[:], T.c[:]).then_inc(T.sem.ldc, 16)
        g.scalar.dma_start(T.xin[:], T.x[:]).then_inc(T.sem.ldx, 16)
        g.vector.wait_ge(T.sem.ldc, 16)
        g.vector.quantize_mx(T.q[:, a:a + WC], T.s[:, a:a + WC], T.cin[:]).then_inc(T.sem.qc, 1)
        g.vector.wait_ge(T.sem.ldx, 16)
        g.vector.quantize_mx(T.q[:, a + WC:a + W], T.s[:, a + WC:a + W], T.xin[:]).then_inc(T.sem.qx, 1)

    sent = 0
    for op in prog.get(core, []):
        if op[0] == "wait":
            for name in op[1]:
                if name == "ownc":
                    g.wait_ge(T.sem.qc, 1)
                elif name == "ownx":
                    g.wait_ge(T.sem.qx, 1)
                else:
                    g.wait_ge(T.sem[name], need[(core, name)])
            continue
        _, kind, t, wave = op
        transfers = []
        for dsts, bl in wave:
            ids = []
            for k in dsts:
                rid, pid, _ = topo.addr(k)
                ids.append(DstId(rid=rid, pnc=pid))
            transfers.append(RemoteDMATransfer(dst_ids=ids, dma_engine_mask=sum(1 << b for b in bl),
                                               remote_sem=T.sem[kind + str(t)], srcs=[view(kind, t)],
                                               dsts=[view(kind, t) for _ in dsts]))
            sent += len(bl)
        g.remote_dma_fused(transfers, local_sem=T.sem.sent)
    if sent:
        g.wait_ge(T.sem.sent, sent)

    if r is None:
        return

    def when(kind, t):
        return 0.0 if t == r else max(est[(core, kind + str(t))], est[(core, "p" + str(t))])

    order = sorted(range(N), key=lambda j: (max(when("x", j), when("a", (r - j) % N)), j))
    seen = set()
    mm = None
    for n, j in enumerate(order):
        k = (r - j) % N
        for name in ("a" + str(k), "p" + str(k), "x" + str(j), "p" + str(j)):
            if name in seen:
                continue
            seen.add(name)
            if name[1:] == str(r):
                g.tensor.wait_ge(T.sem.qc, 1)
                g.tensor.wait_ge(T.sem.qx, 1)
            else:
                g.tensor.wait_ge(T.sem[name], need[(core, name)])
        mm = g.tensor.matmul_mx(T.acc[:, 0:WX], T.q[:, k * W:k * W + WC], T.s[:, k * W:k * W + WC],
                                T.q[:, j * W + WC:(j + 1) * W], T.s[:, j * W + WC:(j + 1) * W], n == 0, n == N - 1)
    mm.then_inc(T.sem.mm, 1)
    g.vector.wait_ge(T.sem.mm, 1)
    g.vector.tensor_copy(T.out[:], T.acc[:, 0:WX]).then_inc(T.sem.cp, 1)
    g.sync.wait_ge(T.sem.cp, 1)
    g.sync.dma_start(T.y[:], T.out[:]).then_inc(T.sem.st, 16)
    g.sync.wait_ge(T.sem.st, 16)
